import numpy as np
import ml_dtypes


def mxq(x, axis, fmt="e4m3"):
    dtype, down = {"e4m3": (ml_dtypes.float8_e4m3fn, 7), "e5m2": (ml_dtypes.float8_e5m2, 14)}[fmt]
    v = np.moveaxis(np.asarray(x, np.float32).astype(ml_dtypes.bfloat16).astype(np.float64), axis, -1)
    blocks = v.reshape(v.shape[:-1] + (-1, 32))
    amax = np.abs(blocks).max(-1, keepdims=True)
    byte = np.maximum(np.where(amax > 0, np.frexp(amax)[1] - 1 + 127, 0) - down, 1)
    scale = np.exp2(byte - 127.0)
    codes = (blocks / scale).astype(np.float32).astype(dtype).astype(np.float64)
    return np.moveaxis((codes * scale).reshape(v.shape), -1, axis)


WIDE = False


def mx_kscale(k):
    if not WIDE:
        return np.ones(k)
    levels = np.array([10, -10, 5, -5, 0])
    if k % 512:
        return np.exp2(np.random.permutation(np.resize(levels, k // 32))).repeat(32)
    a = np.empty((k // 512, 16))
    for p in range(k // 512):
        a[p, :8] = np.random.permutation(np.resize(levels, 8))
        for g in range(8):
            far = levels[np.abs(levels - a[p, g]) >= 10]
            a[p, g + 8] = far[np.random.randint(len(far))]
    return np.exp2(a.ravel()).repeat(32)


BF16 = ml_dtypes.bfloat16


def bf(x):
    return np.asarray(x, np.float32).astype(BF16)


def f64(x):
    return np.asarray(x).astype(np.float64)


E2M1 = np.array([0.0, 0.5, 1.0, 1.5, 2.0, 3.0, 4.0, 6.0, -0.0, -0.5, -1.0, -1.5, -2.0, -3.0, -4.0, -6.0])


def pack_weight(w, fmt):
    k, n = w.shape
    w = f64(bf(w)).reshape(k // 32, 32, n)
    amax = np.abs(w).max(1)
    if fmt == "e4m3":
        byte = np.frexp(amax)[1] - 1 + 127 - 7
    else:
        mant, ex = np.frexp(amax / 6.0)
        byte = np.where(mant > 0.5, ex, ex - 1) + 127
    byte = np.clip(np.where(amax > 0, byte, 1), 1, 254)
    scaled = (w * np.exp2(127.0 - byte)[:, None, :]).reshape(k, n).astype(np.float32)
    by_word = np.ascontiguousarray(scaled.reshape(k // 512, 128, 4, n).transpose(0, 1, 3, 2))
    if fmt == "e4m3":
        words = by_word.astype(ml_dtypes.float8_e4m3fn).view(np.uint8)
    else:
        c = by_word.astype(ml_dtypes.float4_e2m1fn).view(np.uint8) & 0xF
        words = c[..., 0::2] | (c[..., 1::2] << 4)
    return np.ascontiguousarray(words), np.ascontiguousarray(byte.astype(np.uint8).reshape(k // 512, 16, n))


def unpack_weight(words, scales, fmt):
    g, p, n, _ = words.shape
    if fmt == "e4m3":
        vals = np.ascontiguousarray(words).view(ml_dtypes.float8_e4m3fn).astype(np.float64)
    else:
        nib = np.empty((g, p, n, 4), np.uint8)
        nib[..., 0::2] = words & 0xF
        nib[..., 1::2] = words >> 4
        vals = E2M1[nib]
    vals = vals * np.repeat(np.exp2(scales.astype(np.float64) - 127.0), 8, axis=1)[..., None]
    return vals.transpose(0, 1, 3, 2).reshape(g * 512, n)
def pack4(w):
    words, scales = pack_weight(w, "e2m1")
    return words.reshape(words.shape[0], 128, -1), scales


def unpack4(words, scales):
    return unpack_weight(words.reshape(words.shape[0], 128, -1, 2), scales, "e2m1")


D, J, T, L, R = 1024, 512, 1024, 1024, 1024


def draw0():
    s = mx_kscale(J)
    v = mx_kscale(L)
    t = mx_kscale(T)
    phase = np.random.uniform(0.0, 2.0 * np.pi, (D, J))
    cs = np.concatenate([np.cos(phase), np.sin(phase)], axis=0)
    h = np.random.standard_normal((J, T)) * np.sqrt(2.0 / J) / T ** 0.25
    echo = np.random.standard_normal((T, L))
    w = np.random.standard_normal((L, R)) / np.sqrt(L) / T ** 0.25
    taper = np.random.uniform(0.5, 1.5, T)
    w_words, w_scales = pack4(w / v[:, None])
    return {"cs": bf(cs * s),
            "h": bf(h / s[:, None] * t),
            "echo": bf(echo * v),
            "w_words": w_words,
            "w_scales": w_scales,
            "taper": bf(taper / t)}


def core(cs, h, echo, w_words, w_scales, taper):
    f = mxq(f64(cs), 1, "e4m3") @ mxq(f64(h), 0, "e4m3")
    p = mxq(f64(echo), 1, "e4m3") @ unpack4(w_words, w_scales)
    z = p * f64(taper)[:, None]
    y = mxq(f, 1, "e4m3") @ mxq(z, 0, "e4m3")
    e = np.square(y)
    return e[:D] + e[D:]


def e4m3fn_bytes(y):
    return np.clip(np.asarray(y, np.float64), -448.0, 448.0).astype(np.float32).astype(ml_dtypes.float8_e4m3fn).view(np.uint8)


def e4m3fn_values(b):
    return np.asarray(b, np.uint8).view(ml_dtypes.float8_e4m3fn).astype(np.float64)


def setup_inputs():
    d = draw0()
    x0 = np.asarray(d['echo']).astype(np.float64)
    s = (np.max(np.abs(x0), axis=(0,), keepdims=True) / 448.0).astype(np.float32)
    out = {}
    for k, v in d.items():
        if k == 'echo':
            out['echo_bytes'] = e4m3fn_bytes(x0 / s.astype(np.float64))
            out['echo_scale'] = s
        else:
            out[k] = v
    return out


def reference(cs, h, echo_bytes, echo_scale, w_words, w_scales, taper):
    return core(cs, h, e4m3fn_values(echo_bytes) * echo_scale.astype(np.float64), w_words, w_scales, taper)

@@ -1,0 +1,365 @@
+from contextlib import ExitStack
+
+import concourse.mybir as mybir
+from concourse.masks import make_identity
+
+D, J, T, L, R = 1024, 512, 1024, 1024, 1024
+
+F32 = mybir.dt.float32
+BF16 = mybir.dt.bfloat16
+I32 = mybir.dt.int32
+U32 = mybir.dt.uint32
+U8 = mybir.dt.uint8
+FP8 = mybir.dt.float8_e4m3fn
+FP8X4 = mybir.dt.float8_e4m3fn_x4
+FP4X4 = mybir.dt.float4_e2m1fn_x4
+ACT = mybir.ActivationFunctionType
+ALU = mybir.AluOpType
+
+P = 128
+CH = 4
+W512 = 512
+
+FLOPS = 2 * (2 * D * J * T + T * L * R + 2 * D * T * R)
+
+
+def tile_isar_split_real_image_s11_kernel(
+    tc, cs, h, echo_bytes, echo_scale, w_words, w_scales, taper, out
+):
+    nc = tc.nc
+    with ExitStack() as ctx:
+        keep = ctx.enter_context(tc.tile_pool(name="keep", bufs=1))
+        work = ctx.enter_context(tc.tile_pool(name="work", bufs=4))
+        outs = ctx.enter_context(tc.tile_pool(name="outs", bufs=4))
+        psum = ctx.enter_context(tc.psum_pool(name="psum", bufs=8))
+
+        ident = keep.tile([P, P], F32, name="ident", align_bytes=64)
+        scale_p8 = keep.tile([P, 8], F32, name="scale_p8")
+        scale_bc = keep.tile([P, L], F32, name="scale_bc", align_bytes=64)
+        taper_bf = keep.tile([P, 2, 4], BF16, name="taper_bf")
+        taper_f = keep.tile([P, 2, 4], F32, name="taper_f")
+        warm = keep.tile([P, 1], F32, name="warm")
+        cs_raw = [keep.tile([P, 4, J], BF16, name="cs_raw%d" % c, align_bytes=64) for c in range(CH)]
+        cs_grp = [keep.tile([P, W512, 4], BF16, name="cs_grp%d" % c, align_bytes=64) for c in range(CH)]
+        cs_q = [keep.tile([P, W512], U32, name="cs_q%d" % c, align_bytes=64) for c in range(CH)]
+        cs_s = [keep.tile([P, W512], U8, name="cs_s%d" % c, align_bytes=64) for c in range(CH)]
+        h_raw = [keep.tile([P, 4, W512], BF16, name="h_raw%d" % g, align_bytes=64) for g in range(2)]
+        h_grp = [keep.tile([P, W512, 4], BF16, name="h_grp%d" % g, align_bytes=64) for g in range(2)]
+        h_q = [keep.tile([P, W512], U32, name="h_q%d" % g, align_bytes=64) for g in range(2)]
+        h_s = [keep.tile([P, W512], U8, name="h_s%d" % g, align_bytes=64) for g in range(2)]
+        e_bytes = [keep.tile([P, 4, L], U8, name="e_bytes%d" % g, align_bytes=64) for g in range(2)]
+        e_grp = [keep.tile([P, 2, W512, 4], BF16, name="e_grp%d" % g, align_bytes=64) for g in range(2)]
+        e_q = [keep.tile([P, 2, W512], U32, name="e_q%d" % g, align_bytes=64) for g in range(2)]
+        e_s = [keep.tile([P, 2, W512], U8, name="e_s%d" % g, align_bytes=64) for g in range(2)]
+        w_q = keep.tile([P, 2, 2 * R], U8, name="w_q", align_bytes=64)
+        w_s = keep.tile([P, 2, R], U8, name="w_s", align_bytes=64)
+        f_q = [[keep.tile([P, W512], U32, name="f_q%d%d" % (c, g), align_bytes=64) for g in range(2)] for c in range(CH)]
+        f_s = [[keep.tile([P, W512], U8, name="f_s%d%d" % (c, g), align_bytes=64) for g in range(2)] for c in range(CH)]
+        z_q = [[keep.tile([P, W512], U32, name="z_q%d%d" % (g, r), align_bytes=64) for r in range(2)] for g in range(2)]
+        z_s = [[keep.tile([P, W512], U8, name="z_s%d%d" % (g, r), align_bytes=64) for r in range(2)] for g in range(2)]
+        e_sc = {}
+        f_grp = {}
+        z_grp = {}
+        banks = {}
+
+        def bank():
+            t = psum.tile([P, W512], F32, name="bank")
+            return t
+
+        ctx.enter_context(tc.manual_schedule())
+        make_identity(nc, ident[:])
+        nc.gpsimd.memset(w_s[:].bitcast(I32), 0)
+        nc.vector.memset(warm[:], 0.0)
+        nc.scalar.dma_start(out=scale_p8[:], in_=echo_scale.rearrange("o (p c) -> p (o c)", c=8))
+        nc.scalar.dma_start(out=taper_bf[:], in_=taper.rearrange("(g p t) -> p g t", p=P, t=4))
+        nc.scalar.activation(out=warm[:], in_=warm[:], func=ACT.Square)
+
+        def load_cs(c, part):
+            row = part * D + c * 256
+            nc.sync.dma_start(
+                out=cs_raw[c][:, 2 * part : 2 * part + 2, :],
+                in_=cs[row : row + 256, :].rearrange("(p j) k -> p j k", j=2),
+            )
+
+        def load_h(g):
+            nc.sync.dma_start(
+                out=h_raw[g][:],
+                in_=h.rearrange("(p j) w -> p j w", j=4)[:, :, g * W512 : (g + 1) * W512],
+            )
+
+        def load_e(g, half):
+            nc.sync.dma_start(
+                out=e_bytes[g][:, 2 * half : 2 * half + 2, :],
+                in_=echo_bytes[g * W512 : (g + 1) * W512, :].rearrange("(m t) k -> m t k", t=4)[
+                    :, 2 * half : 2 * half + 2, :
+                ],
+            )
+
+        def load_w():
+            nc.sync.dma_start(out=w_q[:].bitcast(I32), in_=w_words.bitcast(I32).rearrange("g p n -> p g n"))
+            for q in range(4):
+                nc.sync.dma_start(
+                    out=w_s[32 * q : 32 * q + 4, :, :].bitcast(I32),
+                    in_=w_scales[:, 4 * q : 4 * q + 4, :].bitcast(I32).rearrange("g q n -> q g n"),
+                )
+
+        load_cs(0, 0)
+        load_cs(0, 1)
+        load_e(0, 0)
+        load_h(0)
+        load_e(0, 1)
+        load_e(1, 0)
+        load_cs(1, 0)
+        load_cs(1, 1)
+        load_e(1, 1)
+        load_h(1)
+        load_cs(2, 0)
+        load_cs(2, 1)
+        load_w()
+        load_cs(3, 0)
+        load_cs(3, 1)
+        nc.vector.tensor_copy(out=taper_f[:], in_=taper_bf[:])
+
+        def scale_spread():
+            for a in range(2):
+                b = bank()
+                for c in range(4):
+                    nc.tensor.transpose(
+                        b[:, c * P : (c + 1) * P],
+                        scale_p8[:, 4 * a + c : 4 * a + c + 1].to_broadcast([P, P]),
+                        ident[:],
+                    )
+                dst = scale_bc[:].rearrange("p (n c) -> p n c", c=8)[:, :, 4 * a : 4 * a + 4]
+                src = b[:].rearrange("p (c n) -> p n c", c=4)
+                if a == 0:
+                    nc.vector.tensor_copy(out=dst, in_=src)
+                else:
+                    nc.scalar.copy(out=dst, in_=src)
+
+        def c_turn(c):
+            for part in range(2):
+                b = bank()
+                banks["c", c, part] = b
+                for j in range(2):
+                    words = cs_raw[c][:, 2 * part + j, :].bitcast(F32)
+                    for u in range(2):
+                        nc.tensor.transpose(
+                            b[:, (2 * j + u) * P : (2 * j + u + 1) * P], words[:, u : 2 * P : 2], ident[:]
+                        )
+
+        def c_out(c):
+            for part in range(2):
+                b = banks["c", c, part]
+                dst = cs_grp[c][:, 256 * part : 256 * part + 256, :].rearrange("p n t -> p (n t)").bitcast(F32)
+                nc.scalar.copy(
+                    out=dst.rearrange("p (j m u) -> p j m u", j=2, u=2),
+                    in_=b[:].rearrange("p (j u m) -> p j m u", j=2, u=2),
+                )
+
+        def c_quant(c):
+            nc.vector.quantize_mx(
+                out=cs_q[c][:].bitcast(FP8X4), scales=cs_s[c][:], in_=cs_grp[c][:].rearrange("p n t -> p (n t)")
+            )
+
+        def h_copy(g, ts):
+            dst = h_grp[g][:].rearrange("p (t m) j -> p t m j", t=4)
+            src = h_raw[g][:].rearrange("p j (m t) -> p t m j", t=4)
+            for t in ts:
+                nc.scalar.copy(out=dst[:, t], in_=src[:, t])
+
+        def h_quant(g):
+            nc.vector.quantize_mx(
+                out=h_q[g][:].bitcast(FP8X4), scales=h_s[g][:], in_=h_grp[g][:].rearrange("p n t -> p (n t)")
+            )
+
+        def e_scale(i):
+            g, t = divmod(i, 4)
+            s = work.tile([P, L], BF16, name="e_sc", bufs=8, align_bytes=64)
+            e_sc[i] = s
+            nc.vector.tensor_tensor(out=s[:], in0=e_bytes[g][:, t, :].bitcast(FP8), in1=scale_bc[:], op=ALU.mult)
+
+        def e_turn(i):
+            b = bank()
+            banks["e", i] = b
+            words = e_sc[i][:].bitcast(F32)
+            for k in range(2):
+                for u in range(2):
+                    nc.tensor.transpose(
+                        b[:, (2 * k + u) * P : (2 * k + u + 1) * P],
+                        words[:, 2 * P * k + u : 2 * P * (k + 1) : 2],
+                        ident[:],
+                    )
+
+        def e_out(i):
+            g, t = divmod(i, 4)
+            b = banks["e", i]
+            dst = e_grp[g][:].rearrange("p k n t -> p (k n t)").bitcast(F32)
+            dst = dst.rearrange("p (k n u) -> p k n u", k=2, u=2)[:, :, t * P : (t + 1) * P, :]
+            nc.scalar.copy(out=dst, in_=b[:].rearrange("p (k u m) -> p k m u", k=2, u=2))
+
+        def e_quant(g):
+            for k in range(2):
+                nc.vector.quantize_mx(
+                    out=e_q[g][:, k, :].bitcast(FP8X4),
+                    scales=e_s[g][:, k, :],
+                    in_=e_grp[g][:, k, :, :].rearrange("p n t -> p (n t)"),
+                )
+
+        def f_mm(c, g, b):
+            t_ = bank()
+            banks["f", c, g, b] = t_
+            cols = slice(b * P, (b + 1) * P)
+            for t in range(4):
+                st = slice(t * P, (t + 1) * P)
+                nc.tensor.matmul_mx(
+                    out=t_[:, st],
+                    lhsT=h_q[g][:, st].bitcast(FP8X4),
+                    lhsT_scale=h_s[g][:, st],
+                    rhs=cs_q[c][:, cols].bitcast(FP8X4),
+                    rhs_scale=cs_s[c][:, cols],
+                    start=True,
+                    stop=True,
+                )
+
+        def f_out(c, g, b, eng):
+            if (c, g) not in f_grp:
+                f_new = work.tile([P, W512, 4], BF16, name="f_grp", bufs=6, align_bytes=64)
+                f_grp[c, g] = f_new
+            dst = f_grp[c, g][:, b * P : (b + 1) * P, :]
+            src = banks["f", c, g, b][:].rearrange("p (t n) -> p n t", t=4)
+            if eng == "v":
+                nc.vector.tensor_copy(out=dst, in_=src)
+            else:
+                nc.scalar.copy(out=dst, in_=src)
+
+        def f_quant(c, g):
+            nc.vector.quantize_mx(
+                out=f_q[c][g][:].bitcast(FP8X4), scales=f_s[c][g][:], in_=f_grp[c, g][:].rearrange("p n t -> p (n t)")
+            )
+
+        def f_bank(c, g, b):
+            f_mm(c, g, b)
+            f_out(c, g, b, "v" if c == 3 or (c == 2 and b % 2 == 1) else "s")
+
+        def z_mm(g, rb):
+            t_ = bank()
+            banks["z", g, rb] = t_
+            cols = slice(rb * P, (rb + 1) * P)
+            for t in range(4):
+                st = slice(t * P, (t + 1) * P)
+                for k in range(2):
+                    nc.tensor.matmul_mx(
+                        out=t_[:, st],
+                        lhsT=e_q[g][:, k, st].bitcast(FP8X4),
+                        lhsT_scale=e_s[g][:, k, st],
+                        rhs=w_q[:, k, 2 * rb * P : 2 * (rb + 1) * P].bitcast(FP4X4),
+                        rhs_scale=w_s[:, k, cols],
+                        start=(k == 0),
+                        stop=(k == 1),
+                    )
+
+        def z_out(g, rb):
+            half, q = divmod(rb, 4)
+            if (g, half) not in z_grp:
+                z_new = work.tile([P, W512, 4], BF16, name="z_grp", align_bytes=64)
+                z_grp[g, half] = z_new
+            nc.vector.tensor_tensor(
+                out=z_grp[g, half][:, q * P : (q + 1) * P, :],
+                in0=banks["z", g, rb][:].rearrange("p (t n) -> p n t", t=4),
+                in1=taper_f[:, g : g + 1, :].to_broadcast([P, P, 4]),
+                op=ALU.mult,
+            )
+
+        def z_quant(g, half):
+            nc.vector.quantize_mx(
+                out=z_q[g][half][:].bitcast(FP8X4),
+                scales=z_s[g][half][:],
+                in_=z_grp[g, half][:].rearrange("p n t -> p (n t)"),
+            )
+
+        def y_unit(c, j, half):
+            sq = []
+            for part in range(2):
+                b = bank()
+                cols = slice((2 * part + j) * P, (2 * part + j + 1) * P)
+                for g in range(2):
+                    nc.tensor.matmul_mx(
+                        out=b[:],
+                        lhsT=f_q[c][g][:, cols].bitcast(FP8X4),
+                        lhsT_scale=f_s[c][g][:, cols],
+                        rhs=z_q[g][half][:].bitcast(FP8X4),
+                        rhs_scale=z_s[g][half][:],
+                        start=(g == 0),
+                        stop=(g == 1),
+                    )
+                s = outs.tile([P, W512], F32, name="sq%d" % part, align_bytes=64)
+                nc.scalar.activation(out=s[:], in_=b[:], func=ACT.Square)
+                sq.append(s)
+            res = outs.tile([P, W512], F32, name="res", align_bytes=64)
+            nc.vector.tensor_tensor(out=res[:], in0=sq[0][:], in1=sq[1][:], op=ALU.add)
+            rows = out[c * 256 : (c + 1) * 256, :].rearrange("(p j) r -> p j r", j=2)
+            nc.sync.dma_start(out=rows[:, j, half * W512 : (half + 1) * W512], in_=res[:])
+
+        scale_spread()
+        for i in range(8):
+            e_scale(i)
+
+        def e_pair(i):
+            for n in (i, i + 1):
+                e_turn(n)
+            for n in (i, i + 1):
+                e_out(n)
+
+        c_turn(0)
+        c_out(0)
+        h_copy(0, (0,))
+        e_pair(0)
+        h_copy(0, (1,))
+        c_turn(1)
+        e_pair(2)
+        c_out(1)
+        e_quant(0)
+        h_copy(0, (2, 3))
+        c_turn(2)
+        e_pair(4)
+        c_out(2)
+        h_copy(1, (0, 1))
+        e_pair(6)
+        c_quant(0)
+        h_quant(0)
+        h_copy(1, (2, 3))
+
+        z_list = [(g, rb) for half in range(2) for g in range(2) for rb in range(4 * half, 4 * half + 4)]
+        f_list = [(c, g, b) for c in range(CH) for g in range(2) for b in range(4)]
+        f_run = (2, 2, 3, 3, 4, 3, 4, 3)
+        after = {
+            2: (lambda: z_quant(0, 0), lambda: f_quant(0, 0)),
+            3: (lambda: z_quant(1, 0), lambda: f_quant(0, 1), lambda: c_quant(2)),
+            4: (lambda: c_turn(3), lambda: c_out(3)),
+            5: (lambda: z_quant(0, 1), lambda: f_quant(1, 0)),
+            6: (lambda: f_quant(1, 1), lambda: c_quant(3)),
+            7: (lambda: f_quant(2, 0), lambda: z_quant(1, 1), lambda: f_quant(2, 1)),
+        }
+        for s in range(8):
+            for z in z_list[2 * s : 2 * s + 2]:
+                z_mm(*z)
+                z_out(*z)
+            if s == 0:
+                e_quant(1)
+            if s == 1:
+                h_quant(1)
+                c_quant(1)
+            for n in range(f_run[s]):
+                f_bank(*f_list[0])
+                f_list = f_list[1:]
+            for step in after.get(s, ()):
+                step()
+        y_list = [(c, j, half) for c, half in ((0, 0), (1, 0), (0, 1), (2, 0), (1, 1), (2, 1), (3, 0), (3, 1)) for j in range(2)]
+        for n, y in enumerate(y_list):
+            y_unit(*y)
+            if n >= 2 and f_list:
+                c, g, b = f_list[0]
+                f_bank(c, g, b)
+                f_list = f_list[1:]
+                if b == 3:
+                    f_quant(c, g)

@@ -34,10 +34,11 @@ def tile_isar_split_real_image_s11_kernel(
         psum = ctx.enter_context(tc.psum_pool(name="psum", bufs=8))
 
         ident = keep.tile([P, P], F32, name="ident", align_bytes=64)
-        scale_p8 = keep.tile([P, 8], F32, name="scale_p8")
+        scale_p8 = keep.tile([P, 2, 4], F32, name="scale_p8")
         scale_bc = keep.tile([P, L], F32, name="scale_bc", align_bytes=64)
         taper_bf = keep.tile([P, 2, 4], BF16, name="taper_bf")
         taper_f = keep.tile([P, 2, 4], F32, name="taper_f")
+        idle = keep.tile([P, W512], BF16, name="idle", align_bytes=64)
         warm = keep.tile([P, 1], F32, name="warm")
         cs_raw = [keep.tile([P, 4, J], BF16, name="cs_raw%d" % c, align_bytes=64) for c in range(CH)]
         cs_grp = [keep.tile([P, W512, 4], BF16, name="cs_grp%d" % c, align_bytes=64) for c in range(CH)]
@@ -70,7 +71,8 @@ def tile_isar_split_real_image_s11_kernel(
         make_identity(nc, ident[:])
         nc.gpsimd.memset(w_s[:].bitcast(I32), 0)
         nc.vector.memset(warm[:], 0.0)
-        nc.scalar.dma_start(out=scale_p8[:], in_=echo_scale.rearrange("o (p c) -> p (o c)", c=8))
+        nc.vector.memset(idle[:], 0.0)
+        nc.scalar.dma_start(out=scale_p8[:], in_=echo_scale.rearrange("o (a p c) -> p (o a) c", a=2, c=4))
         nc.scalar.dma_start(out=taper_bf[:], in_=taper.rearrange("(g p t) -> p g t", p=P, t=4))
         nc.scalar.activation(out=warm[:], in_=warm[:], func=ACT.Square)
 
@@ -103,33 +105,39 @@ def tile_isar_split_real_image_s11_kernel(
                     in_=w_scales[:, 4 * q : 4 * q + 4, :].bitcast(I32).rearrange("g q n -> q g n"),
                 )
 
+        load_e(0, 0)
         load_cs(0, 0)
         load_cs(0, 1)
-        load_e(0, 0)
         load_h(0)
         load_e(0, 1)
         load_e(1, 0)
+        load_e(1, 1)
         load_cs(1, 0)
         load_cs(1, 1)
-        load_e(1, 1)
         load_h(1)
-        load_cs(2, 0)
-        load_cs(2, 1)
         load_w()
-        load_cs(3, 0)
-        load_cs(3, 1)
+        for c in (2, 3):
+            load_cs(c, 0)
+            load_cs(c, 1)
         nc.vector.tensor_copy(out=taper_f[:], in_=taper_bf[:])
+
+        def spin(b, n):
+            for r in range(n):
+                nc.tensor.matmul(out=b[:], lhsT=idle[:, 0:P], rhs=idle[:], start=True, stop=True)
+
+        spins = {("s", 0): 4, ("c", 1): 1, ("e", 0): 2, ("e", 1): 2, ("e", 4): 2, ("e", 5): 2, ("e", 6): 2, ("e", 7): 2}
 
         def scale_spread():
             for a in range(2):
                 b = bank()
+                spin(b, spins.get(("s", a), 0))
                 for c in range(4):
                     nc.tensor.transpose(
                         b[:, c * P : (c + 1) * P],
-                        scale_p8[:, 4 * a + c : 4 * a + c + 1].to_broadcast([P, P]),
+                        scale_p8[:, a, c : c + 1].to_broadcast([P, P]),
                         ident[:],
                     )
-                dst = scale_bc[:].rearrange("p (n c) -> p n c", c=8)[:, :, 4 * a : 4 * a + 4]
+                dst = scale_bc[:, a * W512 : (a + 1) * W512].rearrange("p (n c) -> p n c", c=4)
                 src = b[:].rearrange("p (c n) -> p n c", c=4)
                 if a == 0:
                     nc.vector.tensor_copy(out=dst, in_=src)
@@ -140,6 +148,7 @@ def tile_isar_split_real_image_s11_kernel(
             for part in range(2):
                 b = bank()
                 banks["c", c, part] = b
+                spin(b, spins.get(("c", c), 0) if part == 0 else 0)
                 for j in range(2):
                     words = cs_raw[c][:, 2 * part + j, :].bitcast(F32)
                     for u in range(2):
@@ -176,11 +185,17 @@ def tile_isar_split_real_image_s11_kernel(
             g, t = divmod(i, 4)
             s = work.tile([P, L], BF16, name="e_sc", bufs=8, align_bytes=64)
             e_sc[i] = s
-            nc.vector.tensor_tensor(out=s[:], in0=e_bytes[g][:, t, :].bitcast(FP8), in1=scale_bc[:], op=ALU.mult)
+            width = W512 if i == 0 else L
+            for k in range(0, L, width):
+                ks = slice(k, k + width)
+                nc.vector.tensor_tensor(
+                    out=s[:, ks], in0=e_bytes[g][:, t, ks].bitcast(FP8), in1=scale_bc[:, ks], op=ALU.mult
+                )
 
         def e_turn(i):
             b = bank()
             banks["e", i] = b
+            spin(b, spins.get(("e", i), 0))
             words = e_sc[i][:].bitcast(F32)
             for k in range(2):
                 for u in range(2):
@@ -277,28 +292,32 @@ def tile_isar_split_real_image_s11_kernel(
                 in_=z_grp[g, half][:].rearrange("p n t -> p (n t)"),
             )
 
-        def y_unit(c, j, half):
-            sq = []
-            for part in range(2):
-                b = bank()
-                cols = slice((2 * part + j) * P, (2 * part + j + 1) * P)
-                for g in range(2):
-                    nc.tensor.matmul_mx(
-                        out=b[:],
-                        lhsT=f_q[c][g][:, cols].bitcast(FP8X4),
-                        lhsT_scale=f_s[c][g][:, cols],
-                        rhs=z_q[g][half][:].bitcast(FP8X4),
-                        rhs_scale=z_s[g][half][:],
-                        start=(g == 0),
-                        stop=(g == 1),
-                    )
-                s = outs.tile([P, W512], F32, name="sq%d" % part, align_bytes=64)
-                nc.scalar.activation(out=s[:], in_=b[:], func=ACT.Square)
-                sq.append(s)
-            res = outs.tile([P, W512], F32, name="res", align_bytes=64)
-            nc.vector.tensor_tensor(out=res[:], in0=sq[0][:], in1=sq[1][:], op=ALU.add)
+        def y_unit(c, j, half, pieces=1):
+            width = W512 // pieces
             rows = out[c * 256 : (c + 1) * 256, :].rearrange("(p j) r -> p j r", j=2)
-            nc.sync.dma_start(out=rows[:, j, half * W512 : (half + 1) * W512], in_=res[:])
+            for i in range(pieces):
+                rc = slice(i * width, (i + 1) * width)
+                sq = []
+                for part in range(2):
+                    b = bank()
+                    cols = slice((2 * part + j) * P, (2 * part + j + 1) * P)
+                    for g in range(2):
+                        nc.tensor.matmul_mx(
+                            out=b[:, 0:width],
+                            lhsT=f_q[c][g][:, cols].bitcast(FP8X4),
+                            lhsT_scale=f_s[c][g][:, cols],
+                            rhs=z_q[g][half][:, rc].bitcast(FP8X4),
+                            rhs_scale=z_s[g][half][:, rc],
+                            start=(g == 0),
+                            stop=(g == 1),
+                        )
+                    s = outs.tile([P, W512], F32, name="sq%d" % part, align_bytes=64)
+                    nc.scalar.activation(out=s[:, 0:width], in_=b[:, 0:width], func=ACT.Square)
+                    sq.append(s)
+                res = outs.tile([P, W512], F32, name="res", align_bytes=64)
+                nc.vector.tensor_tensor(out=res[:, 0:width], in0=sq[0][:, 0:width], in1=sq[1][:, 0:width], op=ALU.add)
+                at = half * W512 + i * width
+                nc.sync.dma_start(out=rows[:, j, at : at + width], in_=res[:, 0:width])
 
         scale_spread()
         for i in range(8):
@@ -320,9 +339,7 @@ def tile_isar_split_real_image_s11_kernel(
         c_out(1)
         e_quant(0)
         h_copy(0, (2, 3))
-        c_turn(2)
         e_pair(4)
-        c_out(2)
         h_copy(1, (0, 1))
         e_pair(6)
         c_quant(0)
@@ -333,7 +350,7 @@ def tile_isar_split_real_image_s11_kernel(
         f_list = [(c, g, b) for c in range(CH) for g in range(2) for b in range(4)]
         f_run = (2, 2, 3, 3, 4, 3, 4, 3)
         after = {
-            2: (lambda: z_quant(0, 0), lambda: f_quant(0, 0)),
+            2: (lambda: z_quant(0, 0), lambda: f_quant(0, 0), lambda: c_turn(2), lambda: c_out(2)),
             3: (lambda: z_quant(1, 0), lambda: f_quant(0, 1), lambda: c_quant(2)),
             4: (lambda: c_turn(3), lambda: c_out(3)),
             5: (lambda: z_quant(0, 1), lambda: f_quant(1, 0)),
@@ -356,8 +373,8 @@ def tile_isar_split_real_image_s11_kernel(
                 step()
         y_list = [(c, j, half) for c, half in ((0, 0), (1, 0), (0, 1), (2, 0), (1, 1), (2, 1), (3, 0), (3, 1)) for j in range(2)]
         for n, y in enumerate(y_list):
-            y_unit(*y)
-            if n >= 2 and f_list:
+            y_unit(*y, pieces=2 if n == len(y_list) - 1 else 1)
+            if n >= 1 and f_list:
                 c, g, b = f_list[0]
                 f_bank(c, g, b)
                 f_list = f_list[1:]

@@ -34,6 +34,7 @@ def tile_isar_split_real_image_s11_kernel(
         psum = ctx.enter_context(tc.psum_pool(name="psum", bufs=8))
 
         ident = keep.tile([P, P], F32, name="ident", align_bytes=64)
+        ident_bf = keep.tile([P, P], BF16, name="ident_bf", align_bytes=64)
         scale_p8 = keep.tile([P, 2, 4], F32, name="scale_p8")
         scale_bc = keep.tile([P, L], F32, name="scale_bc", align_bytes=64)
         taper_bf = keep.tile([P, 2, 4], BF16, name="taper_bf")
@@ -69,6 +70,7 @@ def tile_isar_split_real_image_s11_kernel(
 
         ctx.enter_context(tc.manual_schedule())
         make_identity(nc, ident[:])
+        make_identity(nc, ident_bf[:])
         nc.gpsimd.memset(w_s[:].bitcast(I32), 0)
         nc.vector.memset(warm[:], 0.0)
         nc.vector.memset(idle[:], 0.0)
@@ -115,17 +117,18 @@ def tile_isar_split_real_image_s11_kernel(
         load_cs(1, 0)
         load_cs(1, 1)
         load_h(1)
+        load_cs(2, 0)
+        load_cs(2, 1)
         load_w()
-        for c in (2, 3):
-            load_cs(c, 0)
-            load_cs(c, 1)
+        load_cs(3, 0)
+        load_cs(3, 1)
         nc.vector.tensor_copy(out=taper_f[:], in_=taper_bf[:])
 
         def spin(b, n):
             for r in range(n):
                 nc.tensor.matmul(out=b[:], lhsT=idle[:, 0:P], rhs=idle[:], start=True, stop=True)
 
-        spins = {("s", 0): 4, ("c", 1): 1, ("e", 0): 2, ("e", 1): 2, ("e", 4): 2, ("e", 5): 2, ("e", 6): 2, ("e", 7): 2}
+        spins = {("s", 0): 4, ("e", 0): 2, ("e", 1): 1, ("c", 1): 2}
 
         def scale_spread():
             for a in range(2):
@@ -170,11 +173,23 @@ def tile_isar_split_real_image_s11_kernel(
                 out=cs_q[c][:].bitcast(FP8X4), scales=cs_s[c][:], in_=cs_grp[c][:].rearrange("p n t -> p (n t)")
             )
 
-        def h_copy(g, ts):
-            dst = h_grp[g][:].rearrange("p (t m) j -> p t m j", t=4)
-            src = h_raw[g][:].rearrange("p j (m t) -> p t m j", t=4)
-            for t in ts:
-                nc.scalar.copy(out=dst[:, t], in_=src[:, t])
+        def h_pass(g):
+            for half in range(2):
+                b = psum.tile([P, 2 * W512], BF16, name="bank")
+                banks["h", g, half] = b
+                for j in range(4):
+                    nc.tensor.matmul(
+                        out=b[:, 256 * j : 256 * (j + 1)],
+                        lhsT=ident_bf[:],
+                        rhs=h_raw[g][:, j, 256 * half : 256 * (half + 1)],
+                        start=True,
+                        stop=True,
+                    )
+
+        def h_out(g):
+            for half in range(2):
+                dst = h_grp[g][:].rearrange("p (t m) j -> p t m j", t=4)[:, :, 64 * half : 64 * (half + 1), :]
+                nc.scalar.copy(out=dst, in_=banks["h", g, half][:].rearrange("p (j m t) -> p t m j", j=4, t=4))
 
         def h_quant(g):
             nc.vector.quantize_mx(
@@ -254,7 +269,7 @@ def tile_isar_split_real_image_s11_kernel(
 
         def f_bank(c, g, b):
             f_mm(c, g, b)
-            f_out(c, g, b, "v" if c == 3 or (c == 2 and b % 2 == 1) else "s")
+            f_out(c, g, b, "v" if c == 3 or (c == 2 and b == 3) else "s")
 
         def z_mm(g, rb):
             t_ = bank()
@@ -331,47 +346,48 @@ def tile_isar_split_real_image_s11_kernel(
 
         c_turn(0)
         c_out(0)
-        h_copy(0, (0,))
         e_pair(0)
-        h_copy(0, (1,))
-        c_turn(1)
+        h_pass(0)
+        h_out(0)
         e_pair(2)
-        c_out(1)
-        e_quant(0)
-        h_copy(0, (2, 3))
+        c_turn(1)
         e_pair(4)
-        h_copy(1, (0, 1))
+        c_out(1)
+        h_pass(1)
+        h_out(1)
         e_pair(6)
         c_quant(0)
         h_quant(0)
-        h_copy(1, (2, 3))
+        c_turn(2)
+        c_out(2)
+        e_quant(0)
+        h_quant(1)
+        e_quant(1)
 
         z_list = [(g, rb) for half in range(2) for g in range(2) for rb in range(4 * half, 4 * half + 4)]
         f_list = [(c, g, b) for c in range(CH) for g in range(2) for b in range(4)]
-        f_run = (2, 2, 3, 3, 4, 3, 4, 3)
+        f_run = (4, 2, 2, 3, 3, 3, 3, 4)
         after = {
-            2: (lambda: z_quant(0, 0), lambda: f_quant(0, 0), lambda: c_turn(2), lambda: c_out(2)),
-            3: (lambda: z_quant(1, 0), lambda: f_quant(0, 1), lambda: c_quant(2)),
-            4: (lambda: c_turn(3), lambda: c_out(3)),
-            5: (lambda: z_quant(0, 1), lambda: f_quant(1, 0)),
-            6: (lambda: f_quant(1, 1), lambda: c_quant(3)),
-            7: (lambda: f_quant(2, 0), lambda: z_quant(1, 1), lambda: f_quant(2, 1)),
+            1: (lambda: c_quant(1), lambda: c_quant(2), lambda: f_quant(0, 0)),
+            2: (lambda: c_turn(3), lambda: c_out(3), lambda: z_quant(0, 0)),
+            3: (lambda: f_quant(0, 1),),
+            4: (lambda: z_quant(1, 0), lambda: c_quant(3)),
+            5: (lambda: f_quant(1, 0),),
+            6: (lambda: z_quant(0, 1), lambda: f_quant(1, 1)),
         }
         for s in range(8):
-            for z in z_list[2 * s : 2 * s + 2]:
-                z_mm(*z)
-                z_out(*z)
-            if s == 0:
-                e_quant(1)
-            if s == 1:
-                h_quant(1)
-                c_quant(1)
             for n in range(f_run[s]):
                 f_bank(*f_list[0])
                 f_list = f_list[1:]
+            for z in z_list[2 * s : 2 * s + 2]:
+                z_mm(*z)
+                z_out(*z)
             for step in after.get(s, ()):
                 step()
-        y_list = [(c, j, half) for c, half in ((0, 0), (1, 0), (0, 1), (2, 0), (1, 1), (2, 1), (3, 0), (3, 1)) for j in range(2)]
+        z_quant(1, 1)
+        f_quant(2, 0)
+        f_quant(2, 1)
+        y_list = [(c, j, half) for c, half in ((0, 0), (1, 0), (0, 1), (1, 1), (2, 0), (2, 1), (3, 0), (3, 1)) for j in range(2)]
         for n, y in enumerate(y_list):
             y_unit(*y, pieces=2 if n == len(y_list) - 1 else 1)
             if n >= 1 and f_list:

@@ -72,8 +72,8 @@ def tile_isar_split_real_image_s11_kernel(
         make_identity(nc, ident[:])
         make_identity(nc, ident_bf[:])
         nc.gpsimd.memset(w_s[:].bitcast(I32), 0)
-        nc.vector.memset(warm[:], 0.0)
         nc.vector.memset(idle[:], 0.0)
+        nc.vector.memset(warm[:], 0.0)
         nc.scalar.dma_start(out=scale_p8[:], in_=echo_scale.rearrange("o (a p c) -> p (o a) c", a=2, c=4))
         nc.scalar.dma_start(out=taper_bf[:], in_=taper.rearrange("(g p t) -> p g t", p=P, t=4))
         nc.scalar.activation(out=warm[:], in_=warm[:], func=ACT.Square)
@@ -122,13 +122,12 @@ def tile_isar_split_real_image_s11_kernel(
         load_w()
         load_cs(3, 0)
         load_cs(3, 1)
-        nc.vector.tensor_copy(out=taper_f[:], in_=taper_bf[:])
 
         def spin(b, n):
             for r in range(n):
                 nc.tensor.matmul(out=b[:], lhsT=idle[:, 0:P], rhs=idle[:], start=True, stop=True)
 
-        spins = {("s", 0): 4, ("e", 0): 2, ("e", 1): 1, ("c", 1): 2}
+        spins = {("s", 0): 2}
 
         def scale_spread():
             for a in range(2):
@@ -173,8 +172,8 @@ def tile_isar_split_real_image_s11_kernel(
                 out=cs_q[c][:].bitcast(FP8X4), scales=cs_s[c][:], in_=cs_grp[c][:].rearrange("p n t -> p (n t)")
             )
 
-        def h_pass(g):
-            for half in range(2):
+        def h_pass(g, halves=(0, 1)):
+            for half in halves:
                 b = psum.tile([P, 2 * W512], BF16, name="bank")
                 banks["h", g, half] = b
                 for j in range(4):
@@ -186,8 +185,8 @@ def tile_isar_split_real_image_s11_kernel(
                         stop=True,
                     )
 
-        def h_out(g):
-            for half in range(2):
+        def h_out(g, halves=(0, 1)):
+            for half in halves:
                 dst = h_grp[g][:].rearrange("p (t m) j -> p t m j", t=4)[:, :, 64 * half : 64 * (half + 1), :]
                 nc.scalar.copy(out=dst, in_=banks["h", g, half][:].rearrange("p (j m t) -> p t m j", j=4, t=4))
 
@@ -269,7 +268,7 @@ def tile_isar_split_real_image_s11_kernel(
 
         def f_bank(c, g, b):
             f_mm(c, g, b)
-            f_out(c, g, b, "v" if c == 3 or (c == 2 and b == 3) else "s")
+            f_out(c, g, b, "v" if (c == 3 and b > 0) or (c == 2 and b == 3) else "s")
 
         def z_mm(g, rb):
             t_ = bank()
@@ -337,6 +336,7 @@ def tile_isar_split_real_image_s11_kernel(
         scale_spread()
         for i in range(8):
             e_scale(i)
+        nc.vector.tensor_copy(out=taper_f[:], in_=taper_bf[:])
 
         def e_pair(i):
             for n in (i, i + 1):
@@ -346,9 +346,11 @@ def tile_isar_split_real_image_s11_kernel(
 
         c_turn(0)
         c_out(0)
-        e_pair(0)
-        h_pass(0)
-        h_out(0)
+        for i in range(2):
+            h_pass(0, (i,))
+            h_out(0, (i,))
+            e_turn(i)
+            e_out(i)
         e_pair(2)
         c_turn(1)
         e_pair(4)

from contextlib import ExitStack

import concourse.mybir as mybir
from concourse.masks import make_identity

D, J, T, L, R = 1024, 512, 1024, 1024, 1024

F32 = mybir.dt.float32
BF16 = mybir.dt.bfloat16
I32 = mybir.dt.int32
U32 = mybir.dt.uint32
U8 = mybir.dt.uint8
FP8 = mybir.dt.float8_e4m3fn
FP8X4 = mybir.dt.float8_e4m3fn_x4
FP4X4 = mybir.dt.float4_e2m1fn_x4
ACT = mybir.ActivationFunctionType
ALU = mybir.AluOpType

P = 128
CH = 4
W512 = 512

FLOPS = 2 * (2 * D * J * T + T * L * R + 2 * D * T * R)


def tile_isar_split_real_image_s11_kernel(
    tc, cs, h, echo_bytes, echo_scale, w_words, w_scales, taper, out
):
    nc = tc.nc
    with ExitStack() as ctx:
        keep = ctx.enter_context(tc.tile_pool(name="keep", bufs=1))
        work = ctx.enter_context(tc.tile_pool(name="work", bufs=4))
        outs = ctx.enter_context(tc.tile_pool(name="outs", bufs=4))
        psum = ctx.enter_context(tc.psum_pool(name="psum", bufs=8))

        ident = keep.tile([P, P], F32, name="ident", align_bytes=64)
        ident_bf = keep.tile([P, P], BF16, name="ident_bf", align_bytes=64)
        scale_p8 = keep.tile([P, 2, 4], F32, name="scale_p8")
        scale_bc = keep.tile([P, L], F32, name="scale_bc", align_bytes=64)
        taper_bf = keep.tile([P, 2, 4], BF16, name="taper_bf")
        taper_f = keep.tile([P, 2, 4], F32, name="taper_f")
        idle = keep.tile([P, W512], BF16, name="idle", align_bytes=64)
        warm = keep.tile([P, 1], F32, name="warm")
        cs_raw = [keep.tile([P, 4, J], BF16, name="cs_raw%d" % c, align_bytes=64) for c in range(CH)]
        cs_grp = [keep.tile([P, W512, 4], BF16, name="cs_grp%d" % c, align_bytes=64) for c in range(CH)]
        cs_q = [keep.tile([P, W512], U32, name="cs_q%d" % c, align_bytes=64) for c in range(CH)]
        cs_s = [keep.tile([P, W512], U8, name="cs_s%d" % c, align_bytes=64) for c in range(CH)]
        h_raw = [keep.tile([P, 4, W512], BF16, name="h_raw%d" % g, align_bytes=64) for g in range(2)]
        h_grp = [keep.tile([P, W512, 4], BF16, name="h_grp%d" % g, align_bytes=64) for g in range(2)]
        h_q = [keep.tile([P, W512], U32, name="h_q%d" % g, align_bytes=64) for g in range(2)]
        h_s = [keep.tile([P, W512], U8, name="h_s%d" % g, align_bytes=64) for g in range(2)]
        e_bytes = [keep.tile([P, 4, L], U8, name="e_bytes%d" % g, align_bytes=64) for g in range(2)]
        e_grp = [keep.tile([P, 2, W512, 4], BF16, name="e_grp%d" % g, align_bytes=64) for g in range(2)]
        e_q = [keep.tile([P, 2, W512], U32, name="e_q%d" % g, align_bytes=64) for g in range(2)]
        e_s = [keep.tile([P, 2, W512], U8, name="e_s%d" % g, align_bytes=64) for g in range(2)]
        w_q = keep.tile([P, 2, 2 * R], U8, name="w_q", align_bytes=64)
        w_s = keep.tile([P, 2, R], U8, name="w_s", align_bytes=64)
        f_q = [[keep.tile([P, W512], U32, name="f_q%d%d" % (c, g), align_bytes=64) for g in range(2)] for c in range(CH)]
        f_s = [[keep.tile([P, W512], U8, name="f_s%d%d" % (c, g), align_bytes=64) for g in range(2)] for c in range(CH)]
        z_q = [[keep.tile([P, W512], U32, name="z_q%d%d" % (g, r), align_bytes=64) for r in range(2)] for g in range(2)]
        z_s = [[keep.tile([P, W512], U8, name="z_s%d%d" % (g, r), align_bytes=64) for r in range(2)] for g in range(2)]
        e_sc = {}
        f_grp = {}
        z_grp = {}
        banks = {}

        def bank():
            t = psum.tile([P, W512], F32, name="bank")
            return t

        ctx.enter_context(tc.manual_schedule())
        make_identity(nc, ident[:])
        make_identity(nc, ident_bf[:])
        nc.gpsimd.memset(w_s[:].bitcast(I32), 0)
        nc.vector.memset(idle[:], 0.0)
        nc.vector.memset(warm[:], 0.0)
        nc.scalar.dma_start(out=scale_p8[:], in_=echo_scale.rearrange("o (a p c) -> p (o a) c", a=2, c=4))
        nc.scalar.dma_start(out=taper_bf[:], in_=taper.rearrange("(g p t) -> p g t", p=P, t=4))
        nc.scalar.activation(out=warm[:], in_=warm[:], func=ACT.Square)

        def load_cs(c, part):
            row = part * D + c * 256
            nc.sync.dma_start(
                out=cs_raw[c][:, 2 * part : 2 * part + 2, :],
                in_=cs[row : row + 256, :].rearrange("(p j) k -> p j k", j=2),
            )

        def load_h(g):
            nc.sync.dma_start(
                out=h_raw[g][:],
                in_=h.rearrange("(p j) w -> p j w", j=4)[:, :, g * W512 : (g + 1) * W512],
            )

        def load_e(g, half):
            nc.sync.dma_start(
                out=e_bytes[g][:, 2 * half : 2 * half + 2, :],
                in_=echo_bytes[g * W512 : (g + 1) * W512, :].rearrange("(m t) k -> m t k", t=4)[
                    :, 2 * half : 2 * half + 2, :
                ],
            )

        def load_w():
            nc.sync.dma_start(out=w_q[:].bitcast(I32), in_=w_words.bitcast(I32).rearrange("g p n -> p g n"))
            for q in range(4):
                nc.sync.dma_start(
                    out=w_s[32 * q : 32 * q + 4, :, :].bitcast(I32),
                    in_=w_scales[:, 4 * q : 4 * q + 4, :].bitcast(I32).rearrange("g q n -> q g n"),
                )

        load_e(0, 0)
        load_cs(0, 0)
        load_cs(0, 1)
        load_h(0)
        load_e(0, 1)
        load_e(1, 0)
        load_e(1, 1)
        load_cs(1, 0)
        load_cs(1, 1)
        load_h(1)
        load_cs(2, 0)
        load_cs(2, 1)
        load_w()
        load_cs(3, 0)
        load_cs(3, 1)

        def spin(b, n):
            for r in range(n):
                nc.tensor.matmul(out=b[:], lhsT=idle[:, 0:P], rhs=idle[:], start=True, stop=True)

        spins = {("s", 0): 2}

        def scale_spread():
            for a in range(2):
                b = bank()
                spin(b, spins.get(("s", a), 0))
                for c in range(4):
                    nc.tensor.transpose(
                        b[:, c * P : (c + 1) * P],
                        scale_p8[:, a, c : c + 1].to_broadcast([P, P]),
                        ident[:],
                    )
                dst = scale_bc[:, a * W512 : (a + 1) * W512].rearrange("p (n c) -> p n c", c=4)
                src = b[:].rearrange("p (c n) -> p n c", c=4)
                if a == 0:
                    nc.vector.tensor_copy(out=dst, in_=src)
                else:
                    nc.scalar.copy(out=dst, in_=src)

        def c_turn(c):
            for part in range(2):
                b = bank()
                banks["c", c, part] = b
                spin(b, spins.get(("c", c), 0) if part == 0 else 0)
                for j in range(2):
                    words = cs_raw[c][:, 2 * part + j, :].bitcast(F32)
                    for u in range(2):
                        nc.tensor.transpose(
                            b[:, (2 * j + u) * P : (2 * j + u + 1) * P], words[:, u : 2 * P : 2], ident[:]
                        )

        def c_out(c):
            for part in range(2):
                b = banks["c", c, part]
                dst = cs_grp[c][:, 256 * part : 256 * part + 256, :].rearrange("p n t -> p (n t)").bitcast(F32)
                nc.scalar.copy(
                    out=dst.rearrange("p (j m u) -> p j m u", j=2, u=2),
                    in_=b[:].rearrange("p (j u m) -> p j m u", j=2, u=2),
                )

        def c_quant(c):
            nc.vector.quantize_mx(
                out=cs_q[c][:].bitcast(FP8X4), scales=cs_s[c][:], in_=cs_grp[c][:].rearrange("p n t -> p (n t)")
            )

        def h_pass(g, halves=(0, 1)):
            for half in halves:
                b = psum.tile([P, 2 * W512], BF16, name="bank")
                banks["h", g, half] = b
                for j in range(4):
                    nc.tensor.matmul(
                        out=b[:, 256 * j : 256 * (j + 1)],
                        lhsT=ident_bf[:],
                        rhs=h_raw[g][:, j, 256 * half : 256 * (half + 1)],
                        start=True,
                        stop=True,
                    )

        def h_out(g, halves=(0, 1)):
            for half in halves:
                dst = h_grp[g][:].rearrange("p (t m) j -> p t m j", t=4)[:, :, 64 * half : 64 * (half + 1), :]
                nc.scalar.copy(out=dst, in_=banks["h", g, half][:].rearrange("p (j m t) -> p t m j", j=4, t=4))

        def h_quant(g):
            nc.vector.quantize_mx(
                out=h_q[g][:].bitcast(FP8X4), scales=h_s[g][:], in_=h_grp[g][:].rearrange("p n t -> p (n t)")
            )

        def e_scale(i):
            g, t = divmod(i, 4)
            s = work.tile([P, L], BF16, name="e_sc", bufs=8, align_bytes=64)
            e_sc[i] = s
            width = W512 if i == 0 else L
            for k in range(0, L, width):
                ks = slice(k, k + width)
                nc.vector.tensor_tensor(
                    out=s[:, ks], in0=e_bytes[g][:, t, ks].bitcast(FP8), in1=scale_bc[:, ks], op=ALU.mult
                )

        def e_turn(i):
            b = bank()
            banks["e", i] = b
            spin(b, spins.get(("e", i), 0))
            words = e_sc[i][:].bitcast(F32)
            for k in range(2):
                for u in range(2):
                    nc.tensor.transpose(
                        b[:, (2 * k + u) * P : (2 * k + u + 1) * P],
                        words[:, 2 * P * k + u : 2 * P * (k + 1) : 2],
                        ident[:],
                    )

        def e_out(i):
            g, t = divmod(i, 4)
            b = banks["e", i]
            dst = e_grp[g][:].rearrange("p k n t -> p (k n t)").bitcast(F32)
            dst = dst.rearrange("p (k n u) -> p k n u", k=2, u=2)[:, :, t * P : (t + 1) * P, :]
            nc.scalar.copy(out=dst, in_=b[:].rearrange("p (k u m) -> p k m u", k=2, u=2))

        def e_quant(g):
            for k in range(2):
                nc.vector.quantize_mx(
                    out=e_q[g][:, k, :].bitcast(FP8X4),
                    scales=e_s[g][:, k, :],
                    in_=e_grp[g][:, k, :, :].rearrange("p n t -> p (n t)"),
                )

        def f_mm(c, g, b):
            t_ = bank()
            banks["f", c, g, b] = t_
            cols = slice(b * P, (b + 1) * P)
            for t in range(4):
                st = slice(t * P, (t + 1) * P)
                nc.tensor.matmul_mx(
                    out=t_[:, st],
                    lhsT=h_q[g][:, st].bitcast(FP8X4),
                    lhsT_scale=h_s[g][:, st],
                    rhs=cs_q[c][:, cols].bitcast(FP8X4),
                    rhs_scale=cs_s[c][:, cols],
                    start=True,
                    stop=True,
                )

        def f_out(c, g, b, eng):
            if (c, g) not in f_grp:
                f_new = work.tile([P, W512, 4], BF16, name="f_grp", bufs=6, align_bytes=64)
                f_grp[c, g] = f_new
            dst = f_grp[c, g][:, b * P : (b + 1) * P, :]
            src = banks["f", c, g, b][:].rearrange("p (t n) -> p n t", t=4)
            if eng == "v":
                nc.vector.tensor_copy(out=dst, in_=src)
            else:
                nc.scalar.copy(out=dst, in_=src)

        def f_quant(c, g):
            nc.vector.quantize_mx(
                out=f_q[c][g][:].bitcast(FP8X4), scales=f_s[c][g][:], in_=f_grp[c, g][:].rearrange("p n t -> p (n t)")
            )

        def f_bank(c, g, b):
            f_mm(c, g, b)
            f_out(c, g, b, "v" if (c == 3 and b > 0) or (c == 2 and b == 3) else "s")

        def z_mm(g, rb):
            t_ = bank()
            banks["z", g, rb] = t_
            cols = slice(rb * P, (rb + 1) * P)
            for t in range(4):
                st = slice(t * P, (t + 1) * P)
                for k in range(2):
                    nc.tensor.matmul_mx(
                        out=t_[:, st],
                        lhsT=e_q[g][:, k, st].bitcast(FP8X4),
                        lhsT_scale=e_s[g][:, k, st],
                        rhs=w_q[:, k, 2 * rb * P : 2 * (rb + 1) * P].bitcast(FP4X4),
                        rhs_scale=w_s[:, k, cols],
                        start=(k == 0),
                        stop=(k == 1),
                    )

        def z_out(g, rb):
            half, q = divmod(rb, 4)
            if (g, half) not in z_grp:
                z_new = work.tile([P, W512, 4], BF16, name="z_grp", align_bytes=64)
                z_grp[g, half] = z_new
            nc.vector.tensor_tensor(
                out=z_grp[g, half][:, q * P : (q + 1) * P, :],
                in0=banks["z", g, rb][:].rearrange("p (t n) -> p n t", t=4),
                in1=taper_f[:, g : g + 1, :].to_broadcast([P, P, 4]),
                op=ALU.mult,
            )

        def z_quant(g, half):
            nc.vector.quantize_mx(
                out=z_q[g][half][:].bitcast(FP8X4),
                scales=z_s[g][half][:],
                in_=z_grp[g, half][:].rearrange("p n t -> p (n t)"),
            )

        def y_unit(c, j, half, pieces=1):
            width = W512 // pieces
            rows = out[c * 256 : (c + 1) * 256, :].rearrange("(p j) r -> p j r", j=2)
            for i in range(pieces):
                rc = slice(i * width, (i + 1) * width)
                sq = []
                for part in range(2):
                    b = bank()
                    cols = slice((2 * part + j) * P, (2 * part + j + 1) * P)
                    for g in range(2):
                        nc.tensor.matmul_mx(
                            out=b[:, 0:width],
                            lhsT=f_q[c][g][:, cols].bitcast(FP8X4),
                            lhsT_scale=f_s[c][g][:, cols],
                            rhs=z_q[g][half][:, rc].bitcast(FP8X4),
                            rhs_scale=z_s[g][half][:, rc],
                            start=(g == 0),
                            stop=(g == 1),
                        )
                    s = outs.tile([P, W512], F32, name="sq%d" % part, align_bytes=64)
                    nc.scalar.activation(out=s[:, 0:width], in_=b[:, 0:width], func=ACT.Square)
                    sq.append(s)
                res = outs.tile([P, W512], F32, name="res", align_bytes=64)
                nc.vector.tensor_tensor(out=res[:, 0:width], in0=sq[0][:, 0:width], in1=sq[1][:, 0:width], op=ALU.add)
                at = half * W512 + i * width
                nc.sync.dma_start(out=rows[:, j, at : at + width], in_=res[:, 0:width])

        scale_spread()
        for i in range(8):
            e_scale(i)
        nc.vector.tensor_copy(out=taper_f[:], in_=taper_bf[:])

        def e_pair(i):
            for n in (i, i + 1):
                e_turn(n)
            for n in (i, i + 1):
                e_out(n)

        c_turn(0)
        c_out(0)
        for i in range(2):
            h_pass(0, (i,))
            h_out(0, (i,))
            e_turn(i)
            e_out(i)
        e_pair(2)
        c_turn(1)
        e_pair(4)
        c_out(1)
        h_pass(1)
        h_out(1)
        e_pair(6)
        c_quant(0)
        h_quant(0)
        c_turn(2)
        c_out(2)
        e_quant(0)
        h_quant(1)
        e_quant(1)

        z_list = [(g, rb) for half in range(2) for g in range(2) for rb in range(4 * half, 4 * half + 4)]
        f_list = [(c, g, b) for c in range(CH) for g in range(2) for b in range(4)]
        f_run = (4, 2, 2, 3, 3, 3, 3, 4)
        after = {
            1: (lambda: c_quant(1), lambda: c_quant(2), lambda: f_quant(0, 0)),
            2: (lambda: c_turn(3), lambda: c_out(3), lambda: z_quant(0, 0)),
            3: (lambda: f_quant(0, 1),),
            4: (lambda: z_quant(1, 0), lambda: c_quant(3)),
            5: (lambda: f_quant(1, 0),),
            6: (lambda: z_quant(0, 1), lambda: f_quant(1, 1)),
        }
        for s in range(8):
            for n in range(f_run[s]):
                f_bank(*f_list[0])
                f_list = f_list[1:]
            for z in z_list[2 * s : 2 * s + 2]:
                z_mm(*z)
                z_out(*z)
            for step in after.get(s, ()):
                step()
        z_quant(1, 1)
        f_quant(2, 0)
        f_quant(2, 1)
        y_list = [(c, j, half) for c, half in ((0, 0), (1, 0), (0, 1), (1, 1), (2, 0), (2, 1), (3, 0), (3, 1)) for j in range(2)]
        for n, y in enumerate(y_list):
            y_unit(*y, pieces=2 if n == len(y_list) - 1 else 1)
            if n >= 1 and f_list:
                c, g, b = f_list[0]
                f_bank(c, g, b)
                f_list = f_list[1:]
                if b == 3:
                    f_quant(c, g)
